import numpy as np
import ml_dtypes


def mxq(x, axis, fmt="e4m3"):
    dtype, down = {"e4m3": (ml_dtypes.float8_e4m3fn, 7), "e5m2": (ml_dtypes.float8_e5m2, 14)}[fmt]
    v = np.moveaxis(np.asarray(x, np.float32).astype(ml_dtypes.bfloat16).astype(np.float64), axis, -1)
    blocks = v.reshape(v.shape[:-1] + (-1, 32))
    amax = np.abs(blocks).max(-1, keepdims=True)
    byte = np.maximum(np.where(amax > 0, np.frexp(amax)[1] - 1 + 127, 0) - down, 1)
    scale = np.exp2(byte - 127.0)
    codes = (blocks / scale).astype(np.float32).astype(dtype).astype(np.float64)
    return np.moveaxis((codes * scale).reshape(v.shape), -1, axis)


WIDE = False


def mx_kscale(k):
    if not WIDE:
        return np.ones(k)
    levels = np.array([10, -10, 5, -5, 0])
    if k % 512:
        return np.exp2(np.random.permutation(np.resize(levels, k // 32))).repeat(32)
    a = np.empty((k // 512, 16))
    for p in range(k // 512):
        a[p, :8] = np.random.permutation(np.resize(levels, 8))
        for g in range(8):
            far = levels[np.abs(levels - a[p, g]) >= 10]
            a[p, g + 8] = far[np.random.randint(len(far))]
    return np.exp2(a.ravel()).repeat(32)


def f64(x):
    return np.asarray(x).astype(np.float64)


def striped(idx):
    return np.tile(idx.reshape(-1, 16).T, (8, 1)).astype(np.uint16)


def unstriped(offs):
    return offs[:16].T.reshape(-1).astype(np.int64)


E2M1 = np.array([0.0, 0.5, 1.0, 1.5, 2.0, 3.0, 4.0, 6.0, -0.0, -0.5, -1.0, -1.5, -2.0, -3.0, -4.0, -6.0])


def pack_weight(w, fmt):
    k, n = w.shape
    w = f64(np.asarray(w, np.float32).astype(ml_dtypes.bfloat16)).reshape(k // 32, 32, n)
    amax = np.abs(w).max(1)
    if fmt == "e4m3":
        byte = np.frexp(amax)[1] - 1 + 127 - 7
    else:
        mant, ex = np.frexp(amax / 6.0)
        byte = np.where(mant > 0.5, ex, ex - 1) + 127
    byte = np.clip(np.where(amax > 0, byte, 1), 1, 254)
    scaled = (w * np.exp2(127.0 - byte)[:, None, :]).reshape(k, n).astype(np.float32)
    by_word = np.ascontiguousarray(scaled.reshape(k // 512, 128, 4, n).transpose(0, 1, 3, 2))
    if fmt == "e4m3":
        words = by_word.astype(ml_dtypes.float8_e4m3fn).view(np.uint8)
    else:
        c = by_word.astype(ml_dtypes.float4_e2m1fn).view(np.uint8) & 0xF
        words = (c[..., 0::2] | (c[..., 1::2] << 4)).reshape(k // 512, 128, 2 * n)
    return np.ascontiguousarray(words), np.ascontiguousarray(byte.astype(np.uint8).reshape(k // 512, 16, n))


def unpack_weight(words, scales, fmt):
    g, _, n = scales.shape
    words = np.ascontiguousarray(words).reshape(g, 128, n, -1)
    if fmt == "e4m3":
        vals = words.view(ml_dtypes.float8_e4m3fn).astype(np.float64)
    else:
        nib = np.empty((g, 128, n, 4), np.uint8)
        nib[..., 0::2] = words & 0xF
        nib[..., 1::2] = words >> 4
        vals = E2M1[nib]
    vals = vals * np.repeat(np.exp2(scales.astype(np.float64) - 127.0), 8, axis=1)[..., None]
    return vals.transpose(0, 1, 3, 2).reshape(g * 512, n)


def gelu(v):
    return 0.5 * v * (1.0 + np.tanh(np.sqrt(2.0 / np.pi) * (v + 0.044715 * v**3)))


def often(T, S):
    return np.random.permutation(T)[(T * np.random.uniform(0, 1, S) ** 4).astype(np.int64)]


K, H, N, T, S, T2, P = 512, 1536, 512, 2048, 1024, 1024, 512

def setup_inputs():
    n = np.random.standard_normal
    s = mx_kscale(K)[:, None]
    u = mx_kscale(H)[:, None]
    tab_words, tab_scales = pack_weight(n((K, T)) * s, "e4m3")
    tab2_words, tab2_scales = pack_weight(n((K, T2)) * s, "e4m3")
    wm = (n((K, H)) / np.sqrt(K) / s * u.T).astype(np.float32)
    wi_words, wi_scales = pack_weight(n((K, H)) / np.sqrt(K) / s * u.T, "e2m1")
    wg = (n((K, H)) / np.sqrt(K) / s).astype(np.float32)
    wd_words, wd_scales = pack_weight(n((K, H)) / np.sqrt(K) / s, "e4m3")
    wf = (n((H, N)) / np.sqrt(H) / u).astype(np.float32)
    return {"tab_words": tab_words, "tab_scales": tab_scales,
            "offs": striped(np.random.permutation(T)[:S]),
            "pos1": striped(often(S, P)),
            "tab2_words": tab2_words, "tab2_scales": tab2_scales,
            "offs2": striped(np.random.permutation(T2)[:P]),
            "wm": wm, "wi_words": wi_words, "wi_scales": wi_scales,
            "wg": wg, "wd_words": wd_words, "wd_scales": wd_scales, "wf": wf}

def reference(tab_words, tab_scales, offs, pos1, tab2_words, tab2_scales, offs2,
              wm, wi_words, wi_scales, wg, wd_words, wd_scales, wf):
    v = unpack_weight(tab_words, tab_scales, "e4m3")[:, unstriped(offs)]
    v2 = unpack_weight(tab2_words, tab2_scales, "e4m3")[:, unstriped(offs2)]
    x1 = mxq(f64(wm), 0, "e4m3").T @ v
    x2 = unpack_weight(wi_words, wi_scales, "e2m1").T @ v
    b1 = mxq(f64(wg), 0, "e4m3").T @ v2
    b2 = unpack_weight(wd_words, wd_scales, "e4m3").T @ v2
    a1 = x1[:, unstriped(pos1)]
    a2 = x2[:, unstriped(pos1)]
    keep = 1.0 / (1.0 + np.exp(-b1))
    z = keep * a1 + a2 * np.tanh(b2)
    out = mxq(f64(wf), 0, "e4m3").T @ mxq(z, 0, "e4m3")
    return out

@@ -1,0 +1,303 @@
+from contextlib import ExitStack
+
+import concourse.mybir as mybir
+
+K, H, N, T, S, T2, D = 512, 1536, 512, 2048, 1024, 1024, 512
+FLOPS = 2 * K * H * (2 * S + 2 * D) + 2 * H * N * D
+
+F32 = mybir.dt.float32
+BF16 = mybir.dt.bfloat16
+I32 = mybir.dt.int32
+U32 = mybir.dt.uint32
+U16 = mybir.dt.uint16
+U8 = mybir.dt.uint8
+FP8X4 = mybir.dt.float8_e4m3fn_x4
+FP4X4 = mybir.dt.float4_e2m1fn_x4
+ACT = mybir.ActivationFunctionType
+ALU = mybir.AluOpType
+
+P = 128
+PACK = 4
+G = P * PACK
+GROUPS = H // G
+BANK = 512
+HALF = D // 2
+
+
+def tile_list_lineage_fate_scores_kernel(
+    tc, tab_words, tab_scales, offs, pos1, tab2_words, tab2_scales, offs2,
+    wm, wi_words, wi_scales, wg, wd_words, wd_scales, wf, out,
+):
+    nc = tc.nc
+    with ExitStack() as ctx:
+        lists = ctx.enter_context(tc.tile_pool(name="lists", bufs=1))
+        held = ctx.enter_context(tc.tile_pool(name="held", bufs=1))
+        ring = ctx.enter_context(tc.tile_pool(name="ring", bufs=2))
+        psum = ctx.enter_context(tc.psum_pool(name="psum", bufs=8))
+
+        offs_sb = lists.tile([P, S // 16], U16, name="offs_sb")
+        pos_sb = lists.tile([P, D // 16], U16, name="pos_sb")
+        offs2_sb = lists.tile([P, D // 16], U16, name="offs2_sb")
+
+        def staged(name, shape, dtype):
+            return ring.tile(shape, dtype, name=name, tag="stage", bufs=4, align_bytes=64)
+
+        tab2_w = staged("tab2_w", [P, T2], I32)
+        tab2_s = staged("tab2_s", [P, T2], U8)
+        tab_w = staged("tab_w", [P, T], I32)
+        tab_s = staged("tab_s", [P, T], U8)
+        wds_raw = held.tile([P, H // 4], I32, name="wds_raw", align_bytes=64)
+        wis_raw = held.tile([P, H // 4], I32, name="wis_raw", align_bytes=64)
+
+        nc.gpsimd.memset(tab2_s[:].bitcast(I32), 0)
+        nc.vector.memset(wds_raw[:], 0)
+        nc.gpsimd.memset(tab_s[:].bitcast(I32), 0)
+        nc.vector.memset(wis_raw[:], 0)
+
+        warm_in = held.tile([P, 8], F32, name="warm_in")
+        warm_out = held.tile([P, 8], F32, name="warm_out")
+        nc.vector.memset(warm_in[:], 0.0)
+        nc.scalar.activation(warm_out[:], warm_in[:], ACT.Sigmoid)
+
+        def load_scale_rows(engine, plane, scales, row):
+            rows = scales[0].bitcast(I32)
+            for q in range(4):
+                engine.dma_start(out=plane[32 * q + row : 32 * q + row + 4, :], in_=rows[4 * q : 4 * q + 4, :])
+
+        def words(ap):
+            return ap[0].rearrange("p c i -> p (c i)").bitcast(I32)
+
+        nc.sync.dma_start(offs2_sb[:], offs2)
+        nc.sync.dma_start(out=tab2_w[:], in_=words(tab2_words))
+        load_scale_rows(nc.scalar, tab2_s[:].bitcast(I32), tab2_scales, 0)
+
+        wd_raw, wi_raw, w_raw = {}, {}, {}
+
+        def load_wd(g):
+            wd_raw[g] = held.tile([P, G], I32, name="wd_raw", align_bytes=64)
+            nc.sync.dma_start(out=wd_raw[g][:], in_=words(wd_words)[:, G * g : G * (g + 1)])
+
+        def load_wi(g):
+            wi_raw[g] = held.tile([P, G // 2], I32, name="wi_raw", align_bytes=64)
+            nc.sync.dma_start(out=wi_raw[g][:], in_=wi_words[0].bitcast(I32)[:, G // 2 * g : G // 2 * (g + 1)])
+
+        def load_first(name, w, g):
+            raw = staged("w_raw", [P, PACK, G], F32)
+            nc.sync.dma_start(out=raw[:], in_=w[:, G * g : G * (g + 1)].rearrange("(p j) c -> p j c", j=PACK))
+            w_raw[name, g] = raw
+
+        def load_wf(g):
+            raw = staged("wf_raw", [P, PACK, N], F32)
+            rows = wf[G * g : G * (g + 1), :].rearrange("(c t i) n -> i c t n", t=PACK, i=4)
+            for i in range(4):
+                nc.sync.dma_start(out=raw[i:P:4, :, :], in_=rows[i])
+            w_raw["wf", g] = raw
+
+        nc.sync.dma_start(offs_sb[:], offs)
+        nc.sync.dma_start(pos_sb[:], pos1)
+        load_wd(0)
+        load_wi(0)
+        load_scale_rows(nc.scalar, wds_raw[:], wd_scales, 0)
+        nc.sync.dma_start(out=tab_w[:], in_=words(tab_words))
+        load_scale_rows(nc.scalar, tab_s[:].bitcast(I32), tab_scales, 0)
+        load_scale_rows(nc.scalar, wis_raw[:], wi_scales, 0)
+
+        def gather_table(name, tw, ts, offsets):
+            vw = held.tile([P, BANK], U32, name=name + "_w", align_bytes=64)
+            vs = held.tile([P, BANK], U8, name=name + "_s", align_bytes=64)
+            nc.vector.tensor_copy(vw[:], tw[:].bitcast(U32).indirect(offsets))
+            nc.vector.tensor_copy(vs[:], ts[:].indirect(offsets))
+            return vw[:].bitcast(FP8X4), vs[:]
+
+        wd_q, wi_q, w_q = {}, {}, {}
+        wds_q = held.tile([P, H], U8, name="wds_q", align_bytes=64)
+        wis_q = held.tile([P, H], U8, name="wis_q", align_bytes=64)
+
+        def order_wd(g):
+            wd_q[g] = held.tile([P, G], I32, name="wd_q%d" % g, align_bytes=64)
+            nc.vector.tensor_copy(
+                wd_q[g][:].rearrange("p (t c i) -> p t c i", t=PACK, i=4),
+                wd_raw[g][:].rearrange("p (c t i) -> p t c i", t=PACK, i=4),
+            )
+
+        def order_wi(g):
+            wi_q[g] = held.tile([P, 2 * G], U8, name="wi_q%d" % g, align_bytes=64)
+            nc.vector.tensor_copy(
+                wi_q[g][:].bitcast(I32).rearrange("p (t c i) -> p t c i", t=PACK, i=2),
+                wi_raw[g][:].rearrange("p (c t i) -> p t c i", t=PACK, i=2),
+            )
+
+        def order_scales(ws_q, ws_raw):
+            nc.vector.tensor_copy(
+                ws_q[:].bitcast(I32).rearrange("p (g t c) -> p t g c", g=GROUPS, t=PACK),
+                ws_raw[:].rearrange("p (g c t) -> p t g c", g=GROUPS, t=PACK),
+            )
+
+        rounded = {}
+
+        def round_weight(name, g, on_scalar):
+            wide = ring.tile([P, G * PACK], BF16, name="w_bf", bufs=3, align_bytes=64)
+            raw = w_raw[name, g]
+            if name == "wf":
+                dst = wide[:].rearrange("p (c i j) -> p c j i", i=4, j=PACK)
+                src = raw[:].rearrange("p j (c i) -> p c j i", i=4)
+            else:
+                dst = wide[:].rearrange("p (t c i j) -> p t c j i", t=PACK, i=4, j=PACK)
+                src = raw[:].rearrange("p j (c t i) -> p t c j i", t=PACK, i=4)
+            if on_scalar:
+                nc.scalar.copy(dst, src)
+            else:
+                nc.vector.tensor_copy(dst, src)
+            rounded[name, g] = wide
+
+        def quantize_weight(name, g):
+            codes = held.tile([P, G], U32, name="%s_codes%d" % (name, g), align_bytes=64)
+            scales = held.tile([P, G], U8, name="%s_scales%d" % (name, g), align_bytes=64)
+            nc.vector.quantize_mx(out=codes[:].bitcast(FP8X4), scales=scales[:], in_=rounded[name, g][:])
+            w_q[name, g] = (codes, scales)
+
+        def stationary(name, g, t):
+            cols = slice(P * t, P * (t + 1))
+            shared = slice(G * g + P * t, G * g + P * (t + 1))
+            if name == "wd":
+                return wd_q[g][:, cols].bitcast(FP8X4), wds_q[:, shared]
+            if name == "wi":
+                return wi_q[g][:, 2 * P * t : 2 * P * (t + 1)].bitcast(FP4X4), wis_q[:, shared]
+            codes, scales = w_q[name, g]
+            return codes[:, cols].bitcast(FP8X4), scales[:, cols]
+
+        def product(name, g, t, moving):
+            bank = psum.tile([P, BANK], F32, name="bank")
+            lhs, lhs_scale = stationary(name, g, t)
+            nc.tensor.matmul_mx(out=bank[:], lhsT=lhs, lhsT_scale=lhs_scale, rhs=moving[0], rhs_scale=moving[1],
+                                start=True, stop=True)
+            return bank
+
+        def daughter_factor(name, func, g, t):
+            bank = product(name, g, t, v2)
+            factor = ring.tile([P, D], F32, name="factor", bufs=8)
+            nc.scalar.activation(factor[:], bank[:], func)
+            return factor
+
+        def mother_half(name, g, t, h, x):
+            bank = product(name, g, t, v[h])
+            nc.scalar.copy(x[:, BANK * h : BANK * (h + 1)], bank[:])
+
+        def new_x():
+            return ring.tile([P, S], F32, name="x", bufs=8)
+
+        def pick(term, t, x, factor, lo, hi):
+            nc.vector.tensor_tensor(term[:, t, lo:hi], x[:].indirect(pos_sb[:, lo // 16 : hi // 16]),
+                                    factor[:, lo:hi], ALU.mult)
+
+        z_q = {}
+
+        def add_terms(g, term_a, term_b, lo, hi):
+            z = ring.tile([P, (hi - lo) * PACK], BF16, name="z_bf", bufs=2, align_bytes=64)
+            nc.vector.tensor_tensor(
+                z[:].rearrange("p (c i t) -> p c t i", i=4, t=PACK),
+                term_a[:, :, lo:hi].rearrange("p t (c i) -> p c t i", i=4),
+                term_b[:, :, lo:hi].rearrange("p t (c i) -> p c t i", i=4),
+                ALU.add,
+            )
+            return z
+
+        def quantize_z(g, z, lo, hi):
+            codes = held.tile([P, hi - lo], U32, name="z_codes%d_%d" % (g, lo), align_bytes=64)
+            scales = held.tile([P, hi - lo], U8, name="z_scales%d_%d" % (g, lo), align_bytes=64)
+            nc.vector.quantize_mx(out=codes[:].bitcast(FP8X4), scales=scales[:], in_=z[:])
+            for h in range(lo // HALF, hi // HALF):
+                cols = slice(HALF * h - lo, HALF * (h + 1) - lo)
+                z_q[g, h] = (codes[:, cols].bitcast(FP8X4), scales[:, cols])
+
+        v2 = gather_table("v2", tab2_w, tab2_s, offs2_sb[:])
+        order_wd(0)
+        order_scales(wds_q, wds_raw)
+        v = [gather_table("v0", tab_w, tab_s, offs_sb[:, 0:32])]
+        order_scales(wis_q, wis_raw)
+        order_wi(0)
+        v.append(gather_table("v1", tab_w, tab_s, offs_sb[:, 32:64]))
+
+        last = GROUPS - 1
+        for g in range(2):
+            load_first("wm", wm, g)
+            load_first("wg", wg, g)
+        for g in range(GROUPS):
+            term_a = ring.tile([P, PACK, D], F32, name="term_a")
+            term_b = ring.tile([P, PACK, D], F32, name="term_b")
+            if g == 0:
+                factors = [daughter_factor("wd", ACT.Tanh, g, t) for t in range(PACK)]
+                xs = [new_x() for t in range(PACK)]
+                for t in range(PACK):
+                    mother_half("wi", g, t, 0, xs[t])
+                round_weight("wm", g, False)
+                quantize_weight("wm", g)
+                for t in range(PACK):
+                    mother_half("wi", g, t, 1, xs[t])
+                    pick(term_a, t, xs[t], factors[t], 0, D)
+                    if t == 0:
+                        round_weight("wg", g, False)
+                    if t == 1:
+                        quantize_weight("wg", g)
+            else:
+                for t in range(PACK):
+                    factor = daughter_factor("wd", ACT.Tanh, g, t)
+                    x = new_x()
+                    for h in range(2):
+                        mother_half("wi", g, t, h, x)
+                    pick(term_a, t, x, factor, 0, D)
+            if g == 0:
+                load_first("wm", wm, last)
+                load_first("wg", wg, last)
+            if g < last:
+                load_wd(g + 1)
+                load_wi(g + 1)
+                order_wd(g + 1)
+                order_wi(g + 1)
+            for t in range(PACK):
+                x = new_x()
+                for h in range(2):
+                    mother_half("wm", g, t, h, x)
+                factor = daughter_factor("wg", ACT.Sigmoid, g, t)
+                if g < last and t % 2 == 1:
+                    round_weight(("wm", "wg")[t // 2], g + 1, True)
+                    quantize_weight(("wm", "wg")[t // 2], g + 1)
+                if g == last and t == PACK - 1:
+                    round_weight("wf", g, True)
+                    pick(term_b, t, x, factor, 0, HALF)
+                    z0 = add_terms(g, term_a, term_b, 0, HALF)
+                    pick(term_b, t, x, factor, HALF, D)
+                    quantize_weight("wf", g)
+                    quantize_z(g, z0, 0, HALF)
+                    z1 = add_terms(g, term_a, term_b, HALF, D)
+                    quantize_z(g, z1, HALF, D)
+                else:
+                    pick(term_b, t, x, factor, 0, D)
+            if g < last:
+                load_wf(g)
+                if g == last - 1:
+                    load_wf(last)
+                z = add_terms(g, term_a, term_b, 0, D)
+                round_weight("wf", g, False)
+                quantize_z(g, z, 0, D)
+                quantize_weight("wf", g)
+
+        accs = {}
+        for h in range(2):
+            for n in range(N // P):
+                accs[h, n] = psum.tile([P, HALF], F32, name="bank")
+                for g in range(last):
+                    lhs, lhs_scale = stationary("wf", g, n)
+                    nc.tensor.matmul_mx(out=accs[h, n][:], lhsT=lhs, lhsT_scale=lhs_scale, rhs=z_q[g, h][0],
+                                        rhs_scale=z_q[g, h][1], start=(g == 0), stop=False)
+        for h in range(2):
+            for n in range(N // P):
+                lhs, lhs_scale = stationary("wf", last, n)
+                nc.tensor.matmul_mx(out=accs[h, n][:], lhsT=lhs, lhsT_scale=lhs_scale, rhs=z_q[last, h][0],
+                                    rhs_scale=z_q[last, h][1], start=False, stop=True)
+                result = held.tile([P, HALF], F32, name="result%d_%d" % (h, n))
+                if h == 1 and n % 2 == 1:
+                    nc.vector.tensor_copy(result[:], accs[h, n][:])
+                else:
+                    nc.scalar.copy(result[:], accs[h, n][:])
+                nc.sync.dma_start(out=out[P * n : P * (n + 1), HALF * h : HALF * (h + 1)], in_=result[:])

@@ -22,6 +22,8 @@ G = P * PACK
 GROUPS = H // G
 BANK = 512
 HALF = D // 2
+SLOT = {"tab2_w":"s0","tab2_s":"s1","tab_w":"s2","tab_s":"s3","wm0":"s0","wg0":"s1","wm1":"s2","wg1":"s3","wm2":"s2","wg2":"s3","term_a0":"a0","term_b0":"b0","term_a1":"a1","term_b1":"b1","term_a2":"a2","term_b2":"b2","wf0":"s0","wf1":"s1","wf2":"s2"}
+ON_SCALAR = ["wg1","wm2","wg2","wf0","wf1","wf2"]
 
 
 def tile_list_lineage_fate_scores_kernel(
@@ -40,13 +42,13 @@ def tile_list_lineage_fate_scores_kernel(
         offs2_sb = lists.tile([P, D // 16], U16, name="offs2_sb")
 
         def staged(name, shape, dtype):
-            return ring.tile(shape, dtype, name=name, tag="stage", bufs=4, align_bytes=64)
+            return held.tile(shape, dtype, name=name, tag=SLOT[name], align_bytes=64)
 
         tab2_w = staged("tab2_w", [P, T2], I32)
         tab2_s = staged("tab2_s", [P, T2], U8)
         tab_w = staged("tab_w", [P, T], I32)
         tab_s = staged("tab_s", [P, T], U8)
-        wds_raw = held.tile([P, H // 4], I32, name="wds_raw", align_bytes=64)
+        wds_raw = held.tile([P, H // 4], I32, name="wds_raw", tag="v0_w", align_bytes=64)
         wis_raw = held.tile([P, H // 4], I32, name="wis_raw", align_bytes=64)
 
         nc.gpsimd.memset(tab2_s[:].bitcast(I32), 0)
@@ -67,65 +69,68 @@ def tile_list_lineage_fate_scores_kernel(
         def words(ap):
             return ap[0].rearrange("p c i -> p (c i)").bitcast(I32)
 
-        nc.sync.dma_start(offs2_sb[:], offs2)
-        nc.sync.dma_start(out=tab2_w[:], in_=words(tab2_words))
-        load_scale_rows(nc.scalar, tab2_s[:].bitcast(I32), tab2_scales, 0)
-
         wd_raw, wi_raw, w_raw = {}, {}, {}
 
-        def load_wd(g):
-            wd_raw[g] = held.tile([P, G], I32, name="wd_raw", align_bytes=64)
-            nc.sync.dma_start(out=wd_raw[g][:], in_=words(wd_words)[:, G * g : G * (g + 1)])
+        def load_wd(lo, hi):
+            wd_raw[lo] = held.tile([P, G * (hi - lo)], I32, name="wd_raw%d" % lo, align_bytes=64)
+            nc.sync.dma_start(out=wd_raw[lo][:], in_=words(wd_words)[:, G * lo : G * hi])
 
-        def load_wi(g):
-            wi_raw[g] = held.tile([P, G // 2], I32, name="wi_raw", align_bytes=64)
-            nc.sync.dma_start(out=wi_raw[g][:], in_=wi_words[0].bitcast(I32)[:, G // 2 * g : G // 2 * (g + 1)])
+        def load_wi(lo, hi):
+            wi_raw[lo] = held.tile([P, G // 2 * (hi - lo)], I32, name="wi_raw%d" % lo, align_bytes=64)
+            nc.sync.dma_start(out=wi_raw[lo][:], in_=wi_words[0].bitcast(I32)[:, G // 2 * lo : G // 2 * hi])
 
         def load_first(name, w, g):
-            raw = staged("w_raw", [P, PACK, G], F32)
+            raw = staged("%s%d" % (name, g), [P, PACK, G], F32)
             nc.sync.dma_start(out=raw[:], in_=w[:, G * g : G * (g + 1)].rearrange("(p j) c -> p j c", j=PACK))
             w_raw[name, g] = raw
 
         def load_wf(g):
-            raw = staged("wf_raw", [P, PACK, N], F32)
+            raw = staged("wf%d" % g, [P, PACK, N], F32)
             rows = wf[G * g : G * (g + 1), :].rearrange("(c t i) n -> i c t n", t=PACK, i=4)
             for i in range(4):
                 nc.sync.dma_start(out=raw[i:P:4, :, :], in_=rows[i])
             w_raw["wf", g] = raw
 
+        nc.sync.dma_start(offs2_sb[:], offs2)
+        nc.sync.dma_start(out=tab2_w[:], in_=words(tab2_words))
         nc.sync.dma_start(offs_sb[:], offs)
-        nc.sync.dma_start(pos_sb[:], pos1)
-        load_wd(0)
-        load_wi(0)
-        load_scale_rows(nc.scalar, wds_raw[:], wd_scales, 0)
+        load_scale_rows(nc.sync, tab2_s[:].bitcast(I32), tab2_scales, 0)
+        load_wd(0, GROUPS)
         nc.sync.dma_start(out=tab_w[:], in_=words(tab_words))
-        load_scale_rows(nc.scalar, tab_s[:].bitcast(I32), tab_scales, 0)
-        load_scale_rows(nc.scalar, wis_raw[:], wi_scales, 0)
+        load_scale_rows(nc.sync, wds_raw[:], wd_scales, 0)
+        load_wi(0, GROUPS)
+        load_scale_rows(nc.sync, wis_raw[:], wi_scales, 0)
+        load_scale_rows(nc.sync, tab_s[:].bitcast(I32), tab_scales, 0)
+        nc.sync.dma_start(pos_sb[:], pos1)
 
-        def gather_table(name, tw, ts, offsets):
-            vw = held.tile([P, BANK], U32, name=name + "_w", align_bytes=64)
-            vs = held.tile([P, BANK], U8, name=name + "_s", align_bytes=64)
+        def gather_table(name, tw, ts, offsets, count):
+            vw = held.tile([P, count], U32, name=name + "_w", tag=name + "_w", align_bytes=64)
+            vs = held.tile([P, count], U8, name=name + "_s", align_bytes=64)
             nc.vector.tensor_copy(vw[:], tw[:].bitcast(U32).indirect(offsets))
             nc.vector.tensor_copy(vs[:], ts[:].indirect(offsets))
-            return vw[:].bitcast(FP8X4), vs[:]
+            return [(vw[:, c : c + BANK].bitcast(FP8X4), vs[:, c : c + BANK]) for c in range(0, count, BANK)]
 
         wd_q, wi_q, w_q = {}, {}, {}
         wds_q = held.tile([P, H], U8, name="wds_q", align_bytes=64)
         wis_q = held.tile([P, H], U8, name="wis_q", align_bytes=64)
 
-        def order_wd(g):
-            wd_q[g] = held.tile([P, G], I32, name="wd_q%d" % g, align_bytes=64)
+        def order_wd(lo, hi):
+            ordered = held.tile([P, G * (hi - lo)], I32, name="wd_q%d" % lo, align_bytes=64)
             nc.vector.tensor_copy(
-                wd_q[g][:].rearrange("p (t c i) -> p t c i", t=PACK, i=4),
-                wd_raw[g][:].rearrange("p (c t i) -> p t c i", t=PACK, i=4),
+                ordered[:].rearrange("p (g t c i) -> p t g c i", t=PACK, c=32, i=4),
+                wd_raw[lo][:].rearrange("p (g c t i) -> p t g c i", t=PACK, c=32, i=4),
             )
+            for g in range(lo, hi):
+                wd_q[g] = ordered[:, G * (g - lo) : G * (g - lo + 1)]
 
-        def order_wi(g):
-            wi_q[g] = held.tile([P, 2 * G], U8, name="wi_q%d" % g, align_bytes=64)
+        def order_wi(lo, hi):
+            ordered = held.tile([P, 2 * G * (hi - lo)], U8, name="wi_q%d" % lo, align_bytes=64)
             nc.vector.tensor_copy(
-                wi_q[g][:].bitcast(I32).rearrange("p (t c i) -> p t c i", t=PACK, i=2),
-                wi_raw[g][:].rearrange("p (c t i) -> p t c i", t=PACK, i=2),
+                ordered[:].bitcast(I32).rearrange("p (g t c i) -> p t g c i", t=PACK, c=32, i=2),
+                wi_raw[lo][:].rearrange("p (g c t i) -> p t g c i", t=PACK, c=32, i=2),
             )
+            for g in range(lo, hi):
+                wi_q[g] = ordered[:, 2 * G * (g - lo) : 2 * G * (g - lo + 1)]
 
         def order_scales(ws_q, ws_raw):
             nc.vector.tensor_copy(
@@ -135,8 +140,11 @@ def tile_list_lineage_fate_scores_kernel(
 
         rounded = {}
 
-        def round_weight(name, g, on_scalar):
-            wide = ring.tile([P, G * PACK], BF16, name="w_bf", bufs=3, align_bytes=64)
+        def round_weight(name, g):
+            if (name, g) == ("wf", GROUPS - 1):
+                wide = held.tile([P, G * PACK], BF16, name="wf_last_bf", tag="last_bf", align_bytes=64)
+            else:
+                wide = ring.tile([P, G * PACK], BF16, name="w_bf", bufs=2, align_bytes=64)
             raw = w_raw[name, g]
             if name == "wf":
                 dst = wide[:].rearrange("p (c i j) -> p c j i", i=4, j=PACK)
@@ -144,7 +152,7 @@ def tile_list_lineage_fate_scores_kernel(
             else:
                 dst = wide[:].rearrange("p (t c i j) -> p t c j i", t=PACK, i=4, j=PACK)
                 src = raw[:].rearrange("p j (c t i) -> p t c j i", t=PACK, i=4)
-            if on_scalar:
+            if "%s%d" % (name, g) in ON_SCALAR:
                 nc.scalar.copy(dst, src)
             else:
                 nc.vector.tensor_copy(dst, src)
@@ -175,7 +183,7 @@ def tile_list_lineage_fate_scores_kernel(
 
         def daughter_factor(name, func, g, t):
             bank = product(name, g, t, v2)
-            factor = ring.tile([P, D], F32, name="factor", bufs=8)
+            factor = ring.tile([P, D], F32, name="factor", bufs=16)
             nc.scalar.activation(factor[:], bank[:], func)
             return factor
 
@@ -193,7 +201,7 @@ def tile_list_lineage_fate_scores_kernel(
         z_q = {}
 
         def add_terms(g, term_a, term_b, lo, hi):
-            z = ring.tile([P, (hi - lo) * PACK], BF16, name="z_bf", bufs=2, align_bytes=64)
+            z = held.tile([P, (hi - lo) * PACK], BF16, name="z_bf", tag="last_bf" if lo else "z_bf", align_bytes=64)
             nc.vector.tensor_tensor(
                 z[:].rearrange("p (c i t) -> p c t i", i=4, t=PACK),
                 term_a[:, :, lo:hi].rearrange("p t (c i) -> p c t i", i=4),
@@ -210,77 +218,57 @@ def tile_list_lineage_fate_scores_kernel(
                 cols = slice(HALF * h - lo, HALF * (h + 1) - lo)
                 z_q[g, h] = (codes[:, cols].bitcast(FP8X4), scales[:, cols])
 
-        v2 = gather_table("v2", tab2_w, tab2_s, offs2_sb[:])
-        order_wd(0)
+        v2 = gather_table("v2", tab2_w, tab2_s, offs2_sb[:], D)[0]
+        order_wd(0, GROUPS)
         order_scales(wds_q, wds_raw)
-        v = [gather_table("v0", tab_w, tab_s, offs_sb[:, 0:32])]
+        order_wi(0, GROUPS)
         order_scales(wis_q, wis_raw)
-        order_wi(0)
-        v.append(gather_table("v1", tab_w, tab_s, offs_sb[:, 32:64]))
+        v = gather_table("v0", tab_w, tab_s, offs_sb[:], S)
 
         last = GROUPS - 1
-        for g in range(2):
-            load_first("wm", wm, g)
-            load_first("wg", wg, g)
-        for g in range(GROUPS):
-            term_a = ring.tile([P, PACK, D], F32, name="term_a")
-            term_b = ring.tile([P, PACK, D], F32, name="term_b")
-            if g == 0:
-                factors = [daughter_factor("wd", ACT.Tanh, g, t) for t in range(PACK)]
-                xs = [new_x() for t in range(PACK)]
-                for t in range(PACK):
-                    mother_half("wi", g, t, 0, xs[t])
-                round_weight("wm", g, False)
-                quantize_weight("wm", g)
-                for t in range(PACK):
-                    mother_half("wi", g, t, 1, xs[t])
-                    pick(term_a, t, xs[t], factors[t], 0, D)
-                    if t == 0:
-                        round_weight("wg", g, False)
-                    if t == 1:
-                        quantize_weight("wg", g)
-            else:
-                for t in range(PACK):
-                    factor = daughter_factor("wd", ACT.Tanh, g, t)
-                    x = new_x()
-                    for h in range(2):
-                        mother_half("wi", g, t, h, x)
-                    pick(term_a, t, x, factor, 0, D)
-            if g == 0:
-                load_first("wm", wm, last)
-                load_first("wg", wg, last)
-            if g < last:
-                load_wd(g + 1)
-                load_wi(g + 1)
-                order_wd(g + 1)
-                order_wi(g + 1)
+        terms = {}
+
+        def prepare(names):
+            for name, g in names:
+                round_weight(name, g)
+                quantize_weight(name, g)
+
+        def stage(kind, g, factors, between):
+            gate, func, mother = ("wd", ACT.Tanh, "wi") if kind == "a" else ("wg", ACT.Sigmoid, "wm")
+            term = staged("term_%s%d" % (kind, g), [P, PACK, D], F32)
+            terms[kind, g] = term
             for t in range(PACK):
                 x = new_x()
                 for h in range(2):
-                    mother_half("wm", g, t, h, x)
-                factor = daughter_factor("wg", ACT.Sigmoid, g, t)
-                if g < last and t % 2 == 1:
-                    round_weight(("wm", "wg")[t // 2], g + 1, True)
-                    quantize_weight(("wm", "wg")[t // 2], g + 1)
-                if g == last and t == PACK - 1:
-                    round_weight("wf", g, True)
-                    pick(term_b, t, x, factor, 0, HALF)
-                    z0 = add_terms(g, term_a, term_b, 0, HALF)
-                    pick(term_b, t, x, factor, HALF, D)
-                    quantize_weight("wf", g)
+                    mother_half(mother, g, t, h, x)
+                factor = factors[t] if factors else daughter_factor(gate, func, g, t)
+                prepare(between.get(t, []))
+                if kind == "b" and g == last and t == PACK - 1:
+                    pick(term, t, x, factor, 0, HALF)
+                    z0 = add_terms(g, terms["a", g], term, 0, HALF)
+                    pick(term, t, x, factor, HALF, D)
                     quantize_z(g, z0, 0, HALF)
-                    z1 = add_terms(g, term_a, term_b, HALF, D)
+                    z1 = add_terms(g, terms["a", g], term, HALF, D)
                     quantize_z(g, z1, HALF, D)
                 else:
-                    pick(term_b, t, x, factor, 0, D)
-            if g < last:
-                load_wf(g)
-                if g == last - 1:
-                    load_wf(last)
-                z = add_terms(g, term_a, term_b, 0, D)
-                round_weight("wf", g, False)
-                quantize_z(g, z, 0, D)
-                quantize_weight("wf", g)
+                    pick(term, t, x, factor, 0, D)
+            if kind == "b" and g < last:
+                quantize_z(g, add_terms(g, terms["a", g], term, 0, D), 0, D)
+
+        for g in range(2):
+            load_first("wm", wm, g)
+            load_first("wg", wg, g)
+        early = [[daughter_factor("wd", ACT.Tanh, g, t) for t in range(PACK)] for g in range(3)]
+        stage("a", 0, early[0], {0: [("wm", 0)], 2: [("wg", 0)]})
+        stage("a", 1, early[1], {1: [("wm", 1)]})
+        stage("b", 0, None, {1: [("wg", 1)]})
+        load_first("wm", wm, last)
+        load_first("wg", wg, last)
+        stage("a", 2, early[2], {0: [("wm", 2)], 2: [("wg", 2)]})
+        for k in range(GROUPS):
+            load_wf(k)
+        stage("b", 1, None, {2: [("wf", 0)]})
+        stage("b", 2, None, {1: [("wf", 1)], 3: [("wf", 2)]})
 
         accs = {}
         for h in range(2):

@@ -23,7 +23,7 @@ GROUPS = H // G
 BANK = 512
 HALF = D // 2
 SLOT = {"tab2_w":"s0","tab2_s":"s1","tab_w":"s2","tab_s":"s3","wm0":"s0","wg0":"s1","wm1":"s2","wg1":"s3","wm2":"s2","wg2":"s3","term_a0":"a0","term_b0":"b0","term_a1":"a1","term_b1":"b1","term_a2":"a2","term_b2":"b2","wf0":"s0","wf1":"s1","wf2":"s2"}
-ON_SCALAR = ["wg1","wm2","wg2","wf0","wf1","wf2"]
+ON_SCALAR = ["wm2","wg2","wf0","wf1","wf2"]
 
 
 def tile_list_lineage_fate_scores_kernel(
@@ -260,8 +260,8 @@ def tile_list_lineage_fate_scores_kernel(
             load_first("wg", wg, g)
         early = [[daughter_factor("wd", ACT.Tanh, g, t) for t in range(PACK)] for g in range(3)]
         stage("a", 0, early[0], {0: [("wm", 0)], 2: [("wg", 0)]})
-        stage("a", 1, early[1], {1: [("wm", 1)]})
-        stage("b", 0, None, {1: [("wg", 1)]})
+        stage("a", 1, early[1], {1: [("wm", 1)], 3: [("wg", 1)]})
+        stage("b", 0, None, {})
         load_first("wm", wm, last)
         load_first("wg", wg, last)
         stage("a", 2, early[2], {0: [("wm", 2)], 2: [("wg", 2)]})

@@ -18,12 +18,28 @@ ALU = mybir.AluOpType
 
 P = 128
 PACK = 4
+RUN = 4
+RUNS = P // RUN
 G = P * PACK
 GROUPS = H // G
+LAST = GROUPS - 1
 BANK = 512
+BANKS = 8
 HALF = D // 2
-SLOT = {"tab2_w":"s0","tab2_s":"s1","tab_w":"s2","tab_s":"s3","wm0":"s0","wg0":"s1","wm1":"s2","wg1":"s3","wm2":"s2","wg2":"s3","term_a0":"a0","term_b0":"b0","term_a1":"a1","term_b1":"b1","term_a2":"a2","term_b2":"b2","wf0":"s0","wf1":"s1","wf2":"s2"}
-ON_SCALAR = ["wm2","wg2","wf0","wf1","wf2"]
+SIGMOID_COLS = 64
+
+ROUNDINGS = [(name, g) for g in range(GROUPS) for name in ("wm", "wg")] + [("wf", g) for g in range(GROUPS)]
+ON_SCALAR = 4
+
+STAGING = [
+    ["tab2_w", "wm0", "wf0"],
+    ["tab2_s", "wg0", "wf1"],
+    ["tab_w", "wm1", "wm2", "wf2"],
+    ["tab_s", "wg1", "wg2"],
+]
+
+X_TILES = 8
+FACTOR_TILES = (GROUPS + 1) * PACK
 
 
 def tile_list_lineage_fate_scores_kernel(
@@ -35,20 +51,21 @@ def tile_list_lineage_fate_scores_kernel(
         lists = ctx.enter_context(tc.tile_pool(name="lists", bufs=1))
         held = ctx.enter_context(tc.tile_pool(name="held", bufs=1))
         ring = ctx.enter_context(tc.tile_pool(name="ring", bufs=2))
-        psum = ctx.enter_context(tc.psum_pool(name="psum", bufs=8))
+        psum = ctx.enter_context(tc.psum_pool(name="psum", bufs=BANKS))
 
         offs_sb = lists.tile([P, S // 16], U16, name="offs_sb")
         pos_sb = lists.tile([P, D // 16], U16, name="pos_sb")
         offs2_sb = lists.tile([P, D // 16], U16, name="offs2_sb")
 
         def staged(name, shape, dtype):
-            return held.tile(shape, dtype, name=name, tag=SLOT[name], align_bytes=64)
+            buffer = [b for b in range(len(STAGING)) if name in STAGING[b]][0]
+            return held.tile(shape, dtype, name=name, tag="staging%d" % buffer, align_bytes=64)
 
         tab2_w = staged("tab2_w", [P, T2], I32)
         tab2_s = staged("tab2_s", [P, T2], U8)
         tab_w = staged("tab_w", [P, T], I32)
         tab_s = staged("tab_s", [P, T], U8)
-        wds_raw = held.tile([P, H // 4], I32, name="wds_raw", tag="v0_w", align_bytes=64)
+        wds_raw = held.tile([P, H // 4], I32, name="wds_raw", tag="v_w", align_bytes=64)
         wis_raw = held.tile([P, H // 4], I32, name="wis_raw", align_bytes=64)
 
         nc.gpsimd.memset(tab2_s[:].bitcast(I32), 0)
@@ -56,156 +73,145 @@ def tile_list_lineage_fate_scores_kernel(
         nc.gpsimd.memset(tab_s[:].bitcast(I32), 0)
         nc.vector.memset(wis_raw[:], 0)
 
-        warm_in = held.tile([P, 8], F32, name="warm_in")
-        warm_out = held.tile([P, 8], F32, name="warm_out")
-        nc.vector.memset(warm_in[:], 0.0)
-        nc.scalar.activation(warm_out[:], warm_in[:], ACT.Sigmoid)
-
-        def load_scale_rows(engine, plane, scales, row):
+        def load_scale_rows(tile_i32, scales):
             rows = scales[0].bitcast(I32)
             for q in range(4):
-                engine.dma_start(out=plane[32 * q + row : 32 * q + row + 4, :], in_=rows[4 * q : 4 * q + 4, :])
+                nc.sync.dma_start(out=tile_i32[32 * q : 32 * q + 4, :], in_=rows[4 * q : 4 * q + 4, :])
 
-        def words(ap):
-            return ap[0].rearrange("p c i -> p (c i)").bitcast(I32)
+        def words(packed):
+            return packed[0].rearrange("p c i -> p (c i)").bitcast(I32)
 
-        wd_raw, wi_raw, w_raw = {}, {}, {}
-
-        def load_wd(lo, hi):
-            wd_raw[lo] = held.tile([P, G * (hi - lo)], I32, name="wd_raw%d" % lo, align_bytes=64)
-            nc.sync.dma_start(out=wd_raw[lo][:], in_=words(wd_words)[:, G * lo : G * hi])
-
-        def load_wi(lo, hi):
-            wi_raw[lo] = held.tile([P, G // 2 * (hi - lo)], I32, name="wi_raw%d" % lo, align_bytes=64)
-            nc.sync.dma_start(out=wi_raw[lo][:], in_=wi_words[0].bitcast(I32)[:, G // 2 * lo : G // 2 * hi])
-
-        def load_first(name, w, g):
-            raw = staged("%s%d" % (name, g), [P, PACK, G], F32)
-            nc.sync.dma_start(out=raw[:], in_=w[:, G * g : G * (g + 1)].rearrange("(p j) c -> p j c", j=PACK))
-            w_raw[name, g] = raw
-
-        def load_wf(g):
-            raw = staged("wf%d" % g, [P, PACK, N], F32)
-            rows = wf[G * g : G * (g + 1), :].rearrange("(c t i) n -> i c t n", t=PACK, i=4)
-            for i in range(4):
-                nc.sync.dma_start(out=raw[i:P:4, :, :], in_=rows[i])
-            w_raw["wf", g] = raw
+        wd_raw = held.tile([P, H], I32, name="wd_raw", align_bytes=64)
+        wi_raw = held.tile([P, H // 2], I32, name="wi_raw", align_bytes=64)
 
         nc.sync.dma_start(offs2_sb[:], offs2)
         nc.sync.dma_start(out=tab2_w[:], in_=words(tab2_words))
         nc.sync.dma_start(offs_sb[:], offs)
-        load_scale_rows(nc.sync, tab2_s[:].bitcast(I32), tab2_scales, 0)
-        load_wd(0, GROUPS)
+        load_scale_rows(tab2_s[:].bitcast(I32), tab2_scales)
+        nc.sync.dma_start(out=wd_raw[:], in_=words(wd_words))
         nc.sync.dma_start(out=tab_w[:], in_=words(tab_words))
-        load_scale_rows(nc.sync, wds_raw[:], wd_scales, 0)
-        load_wi(0, GROUPS)
-        load_scale_rows(nc.sync, wis_raw[:], wi_scales, 0)
-        load_scale_rows(nc.sync, tab_s[:].bitcast(I32), tab_scales, 0)
+        load_scale_rows(wds_raw[:], wd_scales)
+        nc.sync.dma_start(out=wi_raw[:], in_=wi_words[0].bitcast(I32))
+        load_scale_rows(wis_raw[:], wi_scales)
+        load_scale_rows(tab_s[:].bitcast(I32), tab_scales)
         nc.sync.dma_start(pos_sb[:], pos1)
 
-        def gather_table(name, tw, ts, offsets, count):
-            vw = held.tile([P, count], U32, name=name + "_w", tag=name + "_w", align_bytes=64)
-            vs = held.tile([P, count], U8, name=name + "_s", align_bytes=64)
-            nc.vector.tensor_copy(vw[:], tw[:].bitcast(U32).indirect(offsets))
-            nc.vector.tensor_copy(vs[:], ts[:].indirect(offsets))
-            return [(vw[:, c : c + BANK].bitcast(FP8X4), vs[:, c : c + BANK]) for c in range(0, count, BANK)]
+        raw = {}
 
-        wd_q, wi_q, w_q = {}, {}, {}
-        wds_q = held.tile([P, H], U8, name="wds_q", align_bytes=64)
-        wis_q = held.tile([P, H], U8, name="wis_q", align_bytes=64)
+        def load_first_weights(g):
+            for name, w in (("wm", wm), ("wg", wg)):
+                raw[name, g] = staged("%s%d" % (name, g), [P, PACK, G], F32)
+                columns = w[:, G * g : G * (g + 1)]
+                nc.sync.dma_start(out=raw[name, g][:], in_=columns.rearrange("(p j) c -> p j c", j=PACK))
 
-        def order_wd(lo, hi):
-            ordered = held.tile([P, G * (hi - lo)], I32, name="wd_q%d" % lo, align_bytes=64)
+        def load_wf(g):
+            raw["wf", g] = staged("wf%d" % g, [P, PACK, N], F32)
+            rows = wf[G * g : G * (g + 1), :].rearrange("(c t i) n -> i c t n", t=PACK, i=RUN)
+            for i in range(RUN):
+                nc.sync.dma_start(out=raw["wf", g][i:P:RUN, :, :], in_=rows[i])
+
+        def gather_table(name, table_w, table_s, offsets, count):
+            picked_w = held.tile([P, count], U32, name=name + "_w", tag=name + "_w", align_bytes=64)
+            picked_s = held.tile([P, count], U8, name=name + "_s", align_bytes=64)
+            nc.vector.tensor_copy(picked_w[:], table_w[:].bitcast(U32).indirect(offsets))
+            nc.vector.tensor_copy(picked_s[:], table_s[:].indirect(offsets))
+            return [(picked_w[:, c : c + BANK].bitcast(FP8X4), picked_s[:, c : c + BANK]) for c in range(0, count, BANK)]
+
+        def order_words(ordered_i32, loaded_i32, run_words):
             nc.vector.tensor_copy(
-                ordered[:].rearrange("p (g t c i) -> p t g c i", t=PACK, c=32, i=4),
-                wd_raw[lo][:].rearrange("p (g c t i) -> p t g c i", t=PACK, c=32, i=4),
-            )
-            for g in range(lo, hi):
-                wd_q[g] = ordered[:, G * (g - lo) : G * (g - lo + 1)]
-
-        def order_wi(lo, hi):
-            ordered = held.tile([P, 2 * G * (hi - lo)], U8, name="wi_q%d" % lo, align_bytes=64)
-            nc.vector.tensor_copy(
-                ordered[:].bitcast(I32).rearrange("p (g t c i) -> p t g c i", t=PACK, c=32, i=2),
-                wi_raw[lo][:].rearrange("p (g c t i) -> p t g c i", t=PACK, c=32, i=2),
-            )
-            for g in range(lo, hi):
-                wi_q[g] = ordered[:, 2 * G * (g - lo) : 2 * G * (g - lo + 1)]
-
-        def order_scales(ws_q, ws_raw):
-            nc.vector.tensor_copy(
-                ws_q[:].bitcast(I32).rearrange("p (g t c) -> p t g c", g=GROUPS, t=PACK),
-                ws_raw[:].rearrange("p (g c t) -> p t g c", g=GROUPS, t=PACK),
+                ordered_i32.rearrange("p (g t c i) -> p t g c i", t=PACK, c=RUNS, i=run_words),
+                loaded_i32.rearrange("p (g c t i) -> p t g c i", t=PACK, c=RUNS, i=run_words),
             )
 
-        rounded = {}
+        def order_scales(ordered, loaded_i32):
+            nc.vector.tensor_copy(
+                ordered[:].bitcast(I32).rearrange("p (g t c) -> p t g c", g=GROUPS, t=PACK),
+                loaded_i32.rearrange("p (g c t) -> p t g c", g=GROUPS, t=PACK),
+            )
 
-        def round_weight(name, g):
-            if (name, g) == ("wf", GROUPS - 1):
-                wide = held.tile([P, G * PACK], BF16, name="wf_last_bf", tag="last_bf", align_bytes=64)
+        wd_codes = held.tile([P, H], I32, name="wd_codes", align_bytes=64)
+        wd_planes = held.tile([P, H], U8, name="wd_planes", align_bytes=64)
+        wi_codes = held.tile([P, 2 * H], U8, name="wi_codes", align_bytes=64)
+        wi_planes = held.tile([P, H], U8, name="wi_planes", align_bytes=64)
+        quantised = {}
+
+        def prepare(name, g):
+            if (name, g) == ROUNDINGS[-1]:
+                rounded = held.tile([P, G * PACK], BF16, name="wf_last_bf", tag="last_bf", align_bytes=64)
             else:
-                wide = ring.tile([P, G * PACK], BF16, name="w_bf", bufs=2, align_bytes=64)
-            raw = w_raw[name, g]
+                rounded = ring.tile([P, G * PACK], BF16, name="w_bf", align_bytes=64)
             if name == "wf":
-                dst = wide[:].rearrange("p (c i j) -> p c j i", i=4, j=PACK)
-                src = raw[:].rearrange("p j (c i) -> p c j i", i=4)
+                dst = rounded[:].rearrange("p (m i j) -> p m j i", i=RUN, j=PACK)
+                src = raw[name, g][:].rearrange("p j (m i) -> p m j i", i=RUN)
             else:
-                dst = wide[:].rearrange("p (t c i j) -> p t c j i", t=PACK, i=4, j=PACK)
-                src = raw[:].rearrange("p j (c t i) -> p t c j i", t=PACK, i=4)
-            if "%s%d" % (name, g) in ON_SCALAR:
+                dst = rounded[:].rearrange("p (t c i j) -> p t c j i", t=PACK, i=RUN, j=PACK)
+                src = raw[name, g][:].rearrange("p j (c t i) -> p t c j i", t=PACK, i=RUN)
+            if (name, g) in ROUNDINGS[-ON_SCALAR:]:
                 nc.scalar.copy(dst, src)
             else:
                 nc.vector.tensor_copy(dst, src)
-            rounded[name, g] = wide
-
-        def quantize_weight(name, g):
             codes = held.tile([P, G], U32, name="%s_codes%d" % (name, g), align_bytes=64)
             scales = held.tile([P, G], U8, name="%s_scales%d" % (name, g), align_bytes=64)
-            nc.vector.quantize_mx(out=codes[:].bitcast(FP8X4), scales=scales[:], in_=rounded[name, g][:])
-            w_q[name, g] = (codes, scales)
+            nc.vector.quantize_mx(out=codes[:].bitcast(FP8X4), scales=scales[:], in_=rounded[:])
+            quantised[name, g] = (codes, scales)
 
-        def stationary(name, g, t):
-            cols = slice(P * t, P * (t + 1))
-            shared = slice(G * g + P * t, G * g + P * (t + 1))
+        def stationary(name, g, tile):
+            lo, hi = G * g + P * tile, G * g + P * (tile + 1)
             if name == "wd":
-                return wd_q[g][:, cols].bitcast(FP8X4), wds_q[:, shared]
+                return wd_codes[:, lo:hi].bitcast(FP8X4), wd_planes[:, lo:hi]
             if name == "wi":
-                return wi_q[g][:, 2 * P * t : 2 * P * (t + 1)].bitcast(FP4X4), wis_q[:, shared]
-            codes, scales = w_q[name, g]
-            return codes[:, cols].bitcast(FP8X4), scales[:, cols]
+                return wi_codes[:, 2 * lo : 2 * hi].bitcast(FP4X4), wi_planes[:, lo:hi]
+            codes, scales = quantised[name, g]
+            return codes[:, P * tile : P * (tile + 1)].bitcast(FP8X4), scales[:, P * tile : P * (tile + 1)]
 
-        def product(name, g, t, moving):
+        def matmul(acc, name, g, tile, moving, start, stop):
+            lhs, lhs_scale = stationary(name, g, tile)
+            nc.tensor.matmul_mx(out=acc[:], lhsT=lhs, lhsT_scale=lhs_scale, rhs=moving[0], rhs_scale=moving[1],
+                                start=start, stop=stop)
+
+        def first_product(name, g, t, moving):
             bank = psum.tile([P, BANK], F32, name="bank")
-            lhs, lhs_scale = stationary(name, g, t)
-            nc.tensor.matmul_mx(out=bank[:], lhsT=lhs, lhsT_scale=lhs_scale, rhs=moving[0], rhs_scale=moving[1],
-                                start=True, stop=True)
+            matmul(bank, name, g, t, moving, True, True)
             return bank
 
-        def daughter_factor(name, func, g, t):
-            bank = product(name, g, t, v2)
-            factor = ring.tile([P, D], F32, name="factor", bufs=16)
-            nc.scalar.activation(factor[:], bank[:], func)
+        def tanh_factor(g, t):
+            bank = first_product("wd", g, t, v2)
+            factor = ring.tile([P, D], F32, name="factor", bufs=FACTOR_TILES)
+            done = 0
+            if (g, t) == (0, 0):
+                done = SIGMOID_COLS
+                half_way = held.tile([P, done], F32, name="half_way")
+                nc.scalar.activation(half_way[:], bank[:, :done], ACT.Sigmoid, scale=2.0)
+                nc.vector.tensor_scalar(factor[:, :done], half_way[:], 2.0, -1.0, ALU.mult, ALU.add)
+            nc.scalar.activation(factor[:, done:], bank[:, done:], ACT.Tanh)
             return factor
 
-        def mother_half(name, g, t, h, x):
-            bank = product(name, g, t, v[h])
-            nc.scalar.copy(x[:, BANK * h : BANK * (h + 1)], bank[:])
+        def sigmoid_factor(g, t):
+            bank = first_product("wg", g, t, v2)
+            factor = ring.tile([P, D], F32, name="factor", bufs=FACTOR_TILES)
+            nc.scalar.activation(factor[:], bank[:], ACT.Sigmoid)
+            return factor
 
-        def new_x():
-            return ring.tile([P, S], F32, name="x", bufs=8)
+        def mother_result(name, g, t):
+            x = ring.tile([P, S], F32, name="x", bufs=X_TILES)
+            for h in range(S // BANK):
+                bank = first_product(name, g, t, v[h])
+                nc.scalar.copy(x[:, BANK * h : BANK * (h + 1)], bank[:])
+            return x
 
         def pick(term, t, x, factor, lo, hi):
             nc.vector.tensor_tensor(term[:, t, lo:hi], x[:].indirect(pos_sb[:, lo // 16 : hi // 16]),
                                     factor[:, lo:hi], ALU.mult)
 
+        terms = {}
         z_q = {}
 
-        def add_terms(g, term_a, term_b, lo, hi):
+        def add_terms(g, lo, hi):
             z = held.tile([P, (hi - lo) * PACK], BF16, name="z_bf", tag="last_bf" if lo else "z_bf", align_bytes=64)
             nc.vector.tensor_tensor(
-                z[:].rearrange("p (c i t) -> p c t i", i=4, t=PACK),
-                term_a[:, :, lo:hi].rearrange("p t (c i) -> p c t i", i=4),
-                term_b[:, :, lo:hi].rearrange("p t (c i) -> p c t i", i=4),
+                z[:].rearrange("p (m i t) -> p m t i", i=RUN, t=PACK),
+                terms["wi", g][:, :, lo:hi].rearrange("p t (m i) -> p m t i", i=RUN),
+                terms["wm", g][:, :, lo:hi].rearrange("p t (m i) -> p m t i", i=RUN),
                 ALU.add,
             )
             return z
@@ -218,71 +224,64 @@ def tile_list_lineage_fate_scores_kernel(
                 cols = slice(HALF * h - lo, HALF * (h + 1) - lo)
                 z_q[g, h] = (codes[:, cols].bitcast(FP8X4), scales[:, cols])
 
-        v2 = gather_table("v2", tab2_w, tab2_s, offs2_sb[:], D)[0]
-        order_wd(0, GROUPS)
-        order_scales(wds_q, wds_raw)
-        order_wi(0, GROUPS)
-        order_scales(wis_q, wis_raw)
-        v = gather_table("v0", tab_w, tab_s, offs_sb[:], S)
-
-        last = GROUPS - 1
-        terms = {}
-
-        def prepare(names):
-            for name, g in names:
-                round_weight(name, g)
-                quantize_weight(name, g)
-
-        def stage(kind, g, factors, between):
-            gate, func, mother = ("wd", ACT.Tanh, "wi") if kind == "a" else ("wg", ACT.Sigmoid, "wm")
-            term = staged("term_%s%d" % (kind, g), [P, PACK, D], F32)
-            terms[kind, g] = term
+        def response_stage(g):
+            terms["wi", g] = held.tile([P, PACK, D], F32, name="response%d" % g, align_bytes=64)
             for t in range(PACK):
-                x = new_x()
-                for h in range(2):
-                    mother_half(mother, g, t, h, x)
-                factor = factors[t] if factors else daughter_factor(gate, func, g, t)
-                prepare(between.get(t, []))
-                if kind == "b" and g == last and t == PACK - 1:
-                    pick(term, t, x, factor, 0, HALF)
-                    z0 = add_terms(g, terms["a", g], term, 0, HALF)
-                    pick(term, t, x, factor, HALF, D)
-                    quantize_z(g, z0, 0, HALF)
-                    z1 = add_terms(g, terms["a", g], term, HALF, D)
-                    quantize_z(g, z1, HALF, D)
-                else:
-                    pick(term, t, x, factor, 0, D)
-            if kind == "b" and g < last:
-                quantize_z(g, add_terms(g, terms["a", g], term, 0, D), 0, D)
+                x = mother_result("wi", g, t)
+                if t in (0, 2):
+                    prepare(("wm", "wg")[t // 2], g)
+                pick(terms["wi", g], t, x, tanh_factors[g][t], 0, D)
 
-        for g in range(2):
-            load_first("wm", wm, g)
-            load_first("wg", wg, g)
-        early = [[daughter_factor("wd", ACT.Tanh, g, t) for t in range(PACK)] for g in range(3)]
-        stage("a", 0, early[0], {0: [("wm", 0)], 2: [("wg", 0)]})
-        stage("a", 1, early[1], {1: [("wm", 1)], 3: [("wg", 1)]})
-        stage("b", 0, None, {})
-        load_first("wm", wm, last)
-        load_first("wg", wg, last)
-        stage("a", 2, early[2], {0: [("wm", 2)], 2: [("wg", 2)]})
-        for k in range(GROUPS):
-            load_wf(k)
-        stage("b", 1, None, {2: [("wf", 0)]})
-        stage("b", 2, None, {1: [("wf", 1)], 3: [("wf", 2)]})
+        def memory_stage(g):
+            terms["wm", g] = held.tile([P, PACK, D], F32, name="memory%d" % g, align_bytes=64)
+            for t in range(PACK):
+                x = mother_result("wm", g, t)
+                factor = sigmoid_factor(g, t)
+                if g > 0 and t == 1:
+                    prepare("wf", g - 1)
+                if g < LAST or t < PACK - 1:
+                    pick(terms["wm", g], t, x, factor, 0, D)
+            if g < LAST:
+                quantize_z(g, add_terms(g, 0, D), 0, D)
+            else:
+                prepare("wf", g)
+                pick(terms["wm", g], t, x, factor, 0, HALF)
+                z_first = add_terms(g, 0, HALF)
+                pick(terms["wm", g], t, x, factor, HALF, D)
+                quantize_z(g, z_first, 0, HALF)
+                quantize_z(g, add_terms(g, HALF, D), HALF, D)
+
+        v2 = gather_table("v2", tab2_w, tab2_s, offs2_sb[:], D)[0]
+        order_words(wd_codes[:], wd_raw[:], RUN)
+        order_scales(wd_planes, wds_raw[:])
+        order_words(wi_codes[:].bitcast(I32), wi_raw[:], RUN // 2)
+        order_scales(wi_planes, wis_raw[:])
+        v = gather_table("v", tab_w, tab_s, offs_sb[:], S)
+
+        for g in range(LAST):
+            load_first_weights(g)
+        tanh_factors = [[tanh_factor(g, t) for t in range(PACK)] for g in range(GROUPS)]
+
+        response_stage(0)
+        for g in range(GROUPS):
+            if g < LAST:
+                response_stage(g + 1)
+            if g + 1 == LAST:
+                for k in range(GROUPS):
+                    load_wf(k)
+            memory_stage(g)
+            if g + 2 == LAST:
+                load_first_weights(LAST)
 
         accs = {}
         for h in range(2):
             for n in range(N // P):
                 accs[h, n] = psum.tile([P, HALF], F32, name="bank")
-                for g in range(last):
-                    lhs, lhs_scale = stationary("wf", g, n)
-                    nc.tensor.matmul_mx(out=accs[h, n][:], lhsT=lhs, lhsT_scale=lhs_scale, rhs=z_q[g, h][0],
-                                        rhs_scale=z_q[g, h][1], start=(g == 0), stop=False)
+                for g in range(LAST):
+                    matmul(accs[h, n], "wf", g, n, z_q[g, h], g == 0, False)
         for h in range(2):
             for n in range(N // P):
-                lhs, lhs_scale = stationary("wf", last, n)
-                nc.tensor.matmul_mx(out=accs[h, n][:], lhsT=lhs, lhsT_scale=lhs_scale, rhs=z_q[last, h][0],
-                                    rhs_scale=z_q[last, h][1], start=False, stop=True)
+                matmul(accs[h, n], "wf", LAST, n, z_q[LAST, h], False, True)
                 result = held.tile([P, HALF], F32, name="result%d_%d" % (h, n))
                 if h == 1 and n % 2 == 1:
                     nc.vector.tensor_copy(result[:], accs[h, n][:])

from contextlib import ExitStack

import concourse.mybir as mybir

K, H, N, T, S, T2, D = 512, 1536, 512, 2048, 1024, 1024, 512
FLOPS = 2 * K * H * (2 * S + 2 * D) + 2 * H * N * D

F32 = mybir.dt.float32
BF16 = mybir.dt.bfloat16
I32 = mybir.dt.int32
U32 = mybir.dt.uint32
U16 = mybir.dt.uint16
U8 = mybir.dt.uint8
FP8X4 = mybir.dt.float8_e4m3fn_x4
FP4X4 = mybir.dt.float4_e2m1fn_x4
ACT = mybir.ActivationFunctionType
ALU = mybir.AluOpType

P = 128
PACK = 4
RUN = 4
RUNS = P // RUN
G = P * PACK
GROUPS = H // G
LAST = GROUPS - 1
BANK = 512
BANKS = 8
HALF = D // 2
SIGMOID_COLS = 64

ROUNDINGS = [(name, g) for g in range(GROUPS) for name in ("wm", "wg")] + [("wf", g) for g in range(GROUPS)]
ON_SCALAR = 4

STAGING = [
    ["tab2_w", "wm0", "wf0"],
    ["tab2_s", "wg0", "wf1"],
    ["tab_w", "wm1", "wm2", "wf2"],
    ["tab_s", "wg1", "wg2"],
]

X_TILES = 8
FACTOR_TILES = (GROUPS + 1) * PACK


def tile_list_lineage_fate_scores_kernel(
    tc, tab_words, tab_scales, offs, pos1, tab2_words, tab2_scales, offs2,
    wm, wi_words, wi_scales, wg, wd_words, wd_scales, wf, out,
):
    nc = tc.nc
    with ExitStack() as ctx:
        lists = ctx.enter_context(tc.tile_pool(name="lists", bufs=1))
        held = ctx.enter_context(tc.tile_pool(name="held", bufs=1))
        ring = ctx.enter_context(tc.tile_pool(name="ring", bufs=2))
        psum = ctx.enter_context(tc.psum_pool(name="psum", bufs=BANKS))

        offs_sb = lists.tile([P, S // 16], U16, name="offs_sb")
        pos_sb = lists.tile([P, D // 16], U16, name="pos_sb")
        offs2_sb = lists.tile([P, D // 16], U16, name="offs2_sb")

        def staged(name, shape, dtype):
            buffer = [b for b in range(len(STAGING)) if name in STAGING[b]][0]
            return held.tile(shape, dtype, name=name, tag="staging%d" % buffer, align_bytes=64)

        tab2_w = staged("tab2_w", [P, T2], I32)
        tab2_s = staged("tab2_s", [P, T2], U8)
        tab_w = staged("tab_w", [P, T], I32)
        tab_s = staged("tab_s", [P, T], U8)
        wds_raw = held.tile([P, H // 4], I32, name="wds_raw", tag="v_w", align_bytes=64)
        wis_raw = held.tile([P, H // 4], I32, name="wis_raw", align_bytes=64)

        nc.gpsimd.memset(tab2_s[:].bitcast(I32), 0)
        nc.vector.memset(wds_raw[:], 0)
        nc.gpsimd.memset(tab_s[:].bitcast(I32), 0)
        nc.vector.memset(wis_raw[:], 0)

        def load_scale_rows(tile_i32, scales):
            rows = scales[0].bitcast(I32)
            for q in range(4):
                nc.sync.dma_start(out=tile_i32[32 * q : 32 * q + 4, :], in_=rows[4 * q : 4 * q + 4, :])

        def words(packed):
            return packed[0].rearrange("p c i -> p (c i)").bitcast(I32)

        wd_raw = held.tile([P, H], I32, name="wd_raw", align_bytes=64)
        wi_raw = held.tile([P, H // 2], I32, name="wi_raw", align_bytes=64)

        nc.sync.dma_start(offs2_sb[:], offs2)
        nc.sync.dma_start(out=tab2_w[:], in_=words(tab2_words))
        nc.sync.dma_start(offs_sb[:], offs)
        load_scale_rows(tab2_s[:].bitcast(I32), tab2_scales)
        nc.sync.dma_start(out=wd_raw[:], in_=words(wd_words))
        nc.sync.dma_start(out=tab_w[:], in_=words(tab_words))
        load_scale_rows(wds_raw[:], wd_scales)
        nc.sync.dma_start(out=wi_raw[:], in_=wi_words[0].bitcast(I32))
        load_scale_rows(wis_raw[:], wi_scales)
        load_scale_rows(tab_s[:].bitcast(I32), tab_scales)
        nc.sync.dma_start(pos_sb[:], pos1)

        raw = {}

        def load_first_weights(g):
            for name, w in (("wm", wm), ("wg", wg)):
                raw[name, g] = staged("%s%d" % (name, g), [P, PACK, G], F32)
                columns = w[:, G * g : G * (g + 1)]
                nc.sync.dma_start(out=raw[name, g][:], in_=columns.rearrange("(p j) c -> p j c", j=PACK))

        def load_wf(g):
            raw["wf", g] = staged("wf%d" % g, [P, PACK, N], F32)
            rows = wf[G * g : G * (g + 1), :].rearrange("(c t i) n -> i c t n", t=PACK, i=RUN)
            for i in range(RUN):
                nc.sync.dma_start(out=raw["wf", g][i:P:RUN, :, :], in_=rows[i])

        def gather_table(name, table_w, table_s, offsets, count):
            picked_w = held.tile([P, count], U32, name=name + "_w", tag=name + "_w", align_bytes=64)
            picked_s = held.tile([P, count], U8, name=name + "_s", align_bytes=64)
            nc.vector.tensor_copy(picked_w[:], table_w[:].bitcast(U32).indirect(offsets))
            nc.vector.tensor_copy(picked_s[:], table_s[:].indirect(offsets))
            return [(picked_w[:, c : c + BANK].bitcast(FP8X4), picked_s[:, c : c + BANK]) for c in range(0, count, BANK)]

        def order_words(ordered_i32, loaded_i32, run_words):
            nc.vector.tensor_copy(
                ordered_i32.rearrange("p (g t c i) -> p t g c i", t=PACK, c=RUNS, i=run_words),
                loaded_i32.rearrange("p (g c t i) -> p t g c i", t=PACK, c=RUNS, i=run_words),
            )

        def order_scales(ordered, loaded_i32):
            nc.vector.tensor_copy(
                ordered[:].bitcast(I32).rearrange("p (g t c) -> p t g c", g=GROUPS, t=PACK),
                loaded_i32.rearrange("p (g c t) -> p t g c", g=GROUPS, t=PACK),
            )

        wd_codes = held.tile([P, H], I32, name="wd_codes", align_bytes=64)
        wd_planes = held.tile([P, H], U8, name="wd_planes", align_bytes=64)
        wi_codes = held.tile([P, 2 * H], U8, name="wi_codes", align_bytes=64)
        wi_planes = held.tile([P, H], U8, name="wi_planes", align_bytes=64)
        quantised = {}

        def prepare(name, g):
            if (name, g) == ROUNDINGS[-1]:
                rounded = held.tile([P, G * PACK], BF16, name="wf_last_bf", tag="last_bf", align_bytes=64)
            else:
                rounded = ring.tile([P, G * PACK], BF16, name="w_bf", align_bytes=64)
            if name == "wf":
                dst = rounded[:].rearrange("p (m i j) -> p m j i", i=RUN, j=PACK)
                src = raw[name, g][:].rearrange("p j (m i) -> p m j i", i=RUN)
            else:
                dst = rounded[:].rearrange("p (t c i j) -> p t c j i", t=PACK, i=RUN, j=PACK)
                src = raw[name, g][:].rearrange("p j (c t i) -> p t c j i", t=PACK, i=RUN)
            if (name, g) in ROUNDINGS[-ON_SCALAR:]:
                nc.scalar.copy(dst, src)
            else:
                nc.vector.tensor_copy(dst, src)
            codes = held.tile([P, G], U32, name="%s_codes%d" % (name, g), align_bytes=64)
            scales = held.tile([P, G], U8, name="%s_scales%d" % (name, g), align_bytes=64)
            nc.vector.quantize_mx(out=codes[:].bitcast(FP8X4), scales=scales[:], in_=rounded[:])
            quantised[name, g] = (codes, scales)

        def stationary(name, g, tile):
            lo, hi = G * g + P * tile, G * g + P * (tile + 1)
            if name == "wd":
                return wd_codes[:, lo:hi].bitcast(FP8X4), wd_planes[:, lo:hi]
            if name == "wi":
                return wi_codes[:, 2 * lo : 2 * hi].bitcast(FP4X4), wi_planes[:, lo:hi]
            codes, scales = quantised[name, g]
            return codes[:, P * tile : P * (tile + 1)].bitcast(FP8X4), scales[:, P * tile : P * (tile + 1)]

        def matmul(acc, name, g, tile, moving, start, stop):
            lhs, lhs_scale = stationary(name, g, tile)
            nc.tensor.matmul_mx(out=acc[:], lhsT=lhs, lhsT_scale=lhs_scale, rhs=moving[0], rhs_scale=moving[1],
                                start=start, stop=stop)

        def first_product(name, g, t, moving):
            bank = psum.tile([P, BANK], F32, name="bank")
            matmul(bank, name, g, t, moving, True, True)
            return bank

        def tanh_factor(g, t):
            bank = first_product("wd", g, t, v2)
            factor = ring.tile([P, D], F32, name="factor", bufs=FACTOR_TILES)
            done = 0
            if (g, t) == (0, 0):
                done = SIGMOID_COLS
                half_way = held.tile([P, done], F32, name="half_way")
                nc.scalar.activation(half_way[:], bank[:, :done], ACT.Sigmoid, scale=2.0)
                nc.vector.tensor_scalar(factor[:, :done], half_way[:], 2.0, -1.0, ALU.mult, ALU.add)
            nc.scalar.activation(factor[:, done:], bank[:, done:], ACT.Tanh)
            return factor

        def sigmoid_factor(g, t):
            bank = first_product("wg", g, t, v2)
            factor = ring.tile([P, D], F32, name="factor", bufs=FACTOR_TILES)
            nc.scalar.activation(factor[:], bank[:], ACT.Sigmoid)
            return factor

        def mother_result(name, g, t):
            x = ring.tile([P, S], F32, name="x", bufs=X_TILES)
            for h in range(S // BANK):
                bank = first_product(name, g, t, v[h])
                nc.scalar.copy(x[:, BANK * h : BANK * (h + 1)], bank[:])
            return x

        def pick(term, t, x, factor, lo, hi):
            nc.vector.tensor_tensor(term[:, t, lo:hi], x[:].indirect(pos_sb[:, lo // 16 : hi // 16]),
                                    factor[:, lo:hi], ALU.mult)

        terms = {}
        z_q = {}

        def add_terms(g, lo, hi):
            z = held.tile([P, (hi - lo) * PACK], BF16, name="z_bf", tag="last_bf" if lo else "z_bf", align_bytes=64)
            nc.vector.tensor_tensor(
                z[:].rearrange("p (m i t) -> p m t i", i=RUN, t=PACK),
                terms["wi", g][:, :, lo:hi].rearrange("p t (m i) -> p m t i", i=RUN),
                terms["wm", g][:, :, lo:hi].rearrange("p t (m i) -> p m t i", i=RUN),
                ALU.add,
            )
            return z

        def quantize_z(g, z, lo, hi):
            codes = held.tile([P, hi - lo], U32, name="z_codes%d_%d" % (g, lo), align_bytes=64)
            scales = held.tile([P, hi - lo], U8, name="z_scales%d_%d" % (g, lo), align_bytes=64)
            nc.vector.quantize_mx(out=codes[:].bitcast(FP8X4), scales=scales[:], in_=z[:])
            for h in range(lo // HALF, hi // HALF):
                cols = slice(HALF * h - lo, HALF * (h + 1) - lo)
                z_q[g, h] = (codes[:, cols].bitcast(FP8X4), scales[:, cols])

        def response_stage(g):
            terms["wi", g] = held.tile([P, PACK, D], F32, name="response%d" % g, align_bytes=64)
            for t in range(PACK):
                x = mother_result("wi", g, t)
                if t in (0, 2):
                    prepare(("wm", "wg")[t // 2], g)
                pick(terms["wi", g], t, x, tanh_factors[g][t], 0, D)

        def memory_stage(g):
            terms["wm", g] = held.tile([P, PACK, D], F32, name="memory%d" % g, align_bytes=64)
            for t in range(PACK):
                x = mother_result("wm", g, t)
                factor = sigmoid_factor(g, t)
                if g > 0 and t == 1:
                    prepare("wf", g - 1)
                if g < LAST or t < PACK - 1:
                    pick(terms["wm", g], t, x, factor, 0, D)
            if g < LAST:
                quantize_z(g, add_terms(g, 0, D), 0, D)
            else:
                prepare("wf", g)
                pick(terms["wm", g], t, x, factor, 0, HALF)
                z_first = add_terms(g, 0, HALF)
                pick(terms["wm", g], t, x, factor, HALF, D)
                quantize_z(g, z_first, 0, HALF)
                quantize_z(g, add_terms(g, HALF, D), HALF, D)

        v2 = gather_table("v2", tab2_w, tab2_s, offs2_sb[:], D)[0]
        order_words(wd_codes[:], wd_raw[:], RUN)
        order_scales(wd_planes, wds_raw[:])
        order_words(wi_codes[:].bitcast(I32), wi_raw[:], RUN // 2)
        order_scales(wi_planes, wis_raw[:])
        v = gather_table("v", tab_w, tab_s, offs_sb[:], S)

        for g in range(LAST):
            load_first_weights(g)
        tanh_factors = [[tanh_factor(g, t) for t in range(PACK)] for g in range(GROUPS)]

        response_stage(0)
        for g in range(GROUPS):
            if g < LAST:
                response_stage(g + 1)
            if g + 1 == LAST:
                for k in range(GROUPS):
                    load_wf(k)
            memory_stage(g)
            if g + 2 == LAST:
                load_first_weights(LAST)

        accs = {}
        for h in range(2):
            for n in range(N // P):
                accs[h, n] = psum.tile([P, HALF], F32, name="bank")
                for g in range(LAST):
                    matmul(accs[h, n], "wf", g, n, z_q[g, h], g == 0, False)
        for h in range(2):
            for n in range(N // P):
                matmul(accs[h, n], "wf", LAST, n, z_q[LAST, h], False, True)
                result = held.tile([P, HALF], F32, name="result%d_%d" % (h, n))
                if h == 1 and n % 2 == 1:
                    nc.vector.tensor_copy(result[:], accs[h, n][:])
                else:
                    nc.scalar.copy(result[:], accs[h, n][:])
                nc.sync.dma_start(out=out[P * n : P * (n + 1), HALF * h : HALF * (h + 1)], in_=result[:])
